import numpy as np
import ml_dtypes


def mxq(x, axis, fmt="e4m3"):
    dtype, down = {"e4m3": (ml_dtypes.float8_e4m3fn, 7), "e5m2": (ml_dtypes.float8_e5m2, 14)}[fmt]
    v = np.moveaxis(np.asarray(x, np.float32).astype(ml_dtypes.bfloat16).astype(np.float64), axis, -1)
    blocks = v.reshape(v.shape[:-1] + (-1, 32))
    amax = np.abs(blocks).max(-1, keepdims=True)
    byte = np.maximum(np.where(amax > 0, np.frexp(amax)[1] - 1 + 127, 0) - down, 1)
    scale = np.exp2(byte - 127.0)
    codes = (blocks / scale).astype(np.float32).astype(dtype).astype(np.float64)
    return np.moveaxis((codes * scale).reshape(v.shape), -1, axis)


WIDE = False


def mx_kscale(k):
    if not WIDE:
        return np.ones(k)
    levels = np.array([10, -10, 5, -5, 0])
    if k % 512:
        return np.exp2(np.random.permutation(np.resize(levels, k // 32))).repeat(32)
    a = np.empty((k // 512, 16))
    for p in range(k // 512):
        a[p, :8] = np.random.permutation(np.resize(levels, 8))
        for g in range(8):
            far = levels[np.abs(levels - a[p, g]) >= 10]
            a[p, g + 8] = far[np.random.randint(len(far))]
    return np.exp2(a.ravel()).repeat(32)


BF16 = ml_dtypes.bfloat16


def bf(x):
    return np.asarray(x, np.float32).astype(BF16)


def f64(x):
    return np.asarray(x).astype(np.float64)

def planes(Y):
    n, m = Y.shape
    b = f64(bf(Y)).reshape(n // 32, 32, m)
    amax = np.abs(b).max(1)
    byte = np.clip(np.where(amax > 0, np.frexp(amax)[1] - 1 + 127 - 7, 1), 1, 254)
    codes = (b * np.exp2(127.0 - byte)[:, None, :]).reshape(n, m).astype(np.float32).astype(ml_dtypes.float8_e4m3fn).view(np.uint8)
    words = codes.reshape(n // 512, 128, 4, m).transpose(0, 1, 3, 2)
    return np.ascontiguousarray(words), np.ascontiguousarray(byte.astype(np.uint8).reshape(n // 512, 16, m))


M, K, N = 1024, 1536, 2048
PI = np.pi

def setup_inputs():
    s = mx_kscale(K)
    x = np.random.randn(M, K)
    w = np.random.randn(K, N) / np.sqrt(K)
    inv_length = np.exp(0.3 * np.random.randn(N))
    phase = np.random.uniform(-PI, PI, N)
    amp = np.exp(0.8 * np.random.randn(N))
    return {
        "x": bf(x * s[None, :]),
        "w": bf(w / s[:, None]),
        "inv_length": bf(inv_length),
        "phase": bf(phase),
        "amp": bf(amp),
    }

def reference(x, w, inv_length, phase, amp):
    xq = mxq(f64(x), 1, "e4m3")
    wq = mxq(f64(w), 0, "e4m3")
    p = xq @ wq
    angle = p * f64(inv_length) + f64(phase)
    y = np.cos(angle) * f64(amp)
    Y = y.T
    words, scales = planes(Y)
    return y, words, scales

@@ -1,0 +1,254 @@
+import math
+from contextlib import ExitStack
+
+import concourse.mybir as mybir
+from concourse.masks import make_identity
+
+M, K, N = 1024, 1536, 2048
+FLOPS = 2 * M * K * N
+
+F32 = mybir.dt.float32
+BF16 = mybir.dt.bfloat16
+I32 = mybir.dt.int32
+U32 = mybir.dt.uint32
+U8 = mybir.dt.uint8
+FP8X4 = mybir.dt.float8_e4m3fn_x4
+ALU = mybir.AluOpType
+ACT = mybir.ActivationFunctionType
+
+P = 128
+PACK = 4
+SPAN = P * PACK
+PASSES = K // SPAN
+GROUPS = N // SPAN
+HALVES = M // SPAN
+UNITS = [(g, h * SPAN, SPAN) for g in range(GROUPS) for h in range(HALVES)][:-1] + [(3, 512, 256), (3, 768, 128), (3, 896, 128)]
+W_STEP = {0: [(1, 0, 88)], 1: [(1, 1, 88), (1, 2, 88)], 2: [(2, 0, 88)], 3: [(2, 1, 88), (2, 2, 88)], 4: [(3, 0, 88)],
+          5: [(3, 1, 88), (3, 2, 88)]}
+TWO_PI = 2.0 * math.pi
+HEAD_SPLIT = (72, 72, 84)
+
+
+def tile_multiscale_random_cosine_features_g1_kernel(tc, x, w, inv_length, phase, amp, out_0, out_1, out_2):
+    nc = tc.nc
+    with ExitStack() as ctx:
+        keep = ctx.enter_context(tc.tile_pool(name="keep", bufs=1))
+        work = ctx.enter_context(tc.tile_pool(name="work", bufs=2))
+        psum = ctx.enter_context(tc.psum_pool(name="psum", bufs=4))
+
+        tiles = {}
+
+        x_codes = keep.tile([P, PASSES, M], U32, name="x_codes", align_bytes=64)
+        x_scales = keep.tile([P, PASSES, M], U8, name="x_scales", align_bytes=64)
+        w_codes = keep.tile([P, GROUPS, PASSES, SPAN], U32, name="w_codes", align_bytes=64)
+        w_scales = keep.tile([P, GROUPS, PASSES, SPAN], U8, name="w_scales", align_bytes=64)
+        y_scales = keep.tile([P, GROUPS, M], U8, name="y_scales", align_bytes=64)
+
+        def load_x(h, c):
+            raw = keep.tile([P, PACK, SPAN], BF16, name="x_raw_%d_%d" % (h, c))
+            src = x[h * SPAN : (h + 1) * SPAN, c * SPAN : (c + 1) * SPAN]
+            nc.sync.dma_start(out=raw[:], in_=src.rearrange("(i p) k -> p i k", p=P))
+            tiles["x_raw", h, c] = raw
+
+        def load_w(g, c):
+            raw = keep.tile([P, PACK, SPAN], BF16, name="w_raw_%d_%d" % (g, c))
+            src = w[c * SPAN : (c + 1) * SPAN, g * SPAN : (g + 1) * SPAN]
+            nc.sync.dma_start(out=raw[:], in_=src.rearrange("(p j) n -> p j n", j=PACK))
+            tiles["w_raw", g, c] = raw
+
+        def load_vector(vec, name):
+            raw = keep.tile([P, GROUPS, PACK], BF16, name=name)
+            nc.scalar.dma_start(out=raw[:], in_=vec.rearrange("(g p t) -> p g t", p=P, t=PACK))
+            return raw[:].rearrange("p g t -> p (g t)")
+
+        def prepare_x(h, c):
+            words = tiles["x_raw", h, c][:].bitcast(F32)
+            grp = work.tile([P, SPAN * PACK], BF16, name="x_grp", bufs=3, align_bytes=64)
+            for pair in range(2):
+                bank = psum.tile([P, 2, 2, P], F32, name="turned", tag="turned")
+                for i in range(2):
+                    for u in range(2):
+                        nc.tensor.transpose(bank[:, i, u, :], words[:, 2 * pair + i, u : 2 * P : 2], ident[:])
+                dst = grp[:].bitcast(F32)[:, pair * SPAN : (pair + 1) * SPAN]
+                nc.scalar.copy(
+                    out=dst.rearrange("p (i r u) -> p i r u", i=2, u=2), in_=bank[:].rearrange("p i u r -> p i r u")
+                )
+            tiles["x_grp", h, c] = grp
+
+        def quant_x(h, c):
+            cols = slice(h * SPAN, (h + 1) * SPAN)
+            nc.vector.quantize_mx(
+                out=x_codes[:, c, cols].bitcast(FP8X4), scales=x_scales[:, c, cols], in_=tiles["x_grp", h, c][:]
+            )
+
+        def group_w(g, c, engine, m0, m1):
+            if ("w_grp", g, c) not in tiles:
+                tiles["w_grp", g, c] = work.tile([P, SPAN * PACK], BF16, name="w_grp", bufs=4, align_bytes=64)
+            dst = tiles["w_grp", g, c][:].rearrange("p (t m j) -> p m t j", t=PACK, j=PACK)[:, m0:m1]
+            src = tiles["w_raw", g, c][:].rearrange("p j (m t) -> p m t j", t=PACK)[:, m0:m1]
+            if engine == "vector":
+                nc.vector.tensor_copy(out=dst, in_=src)
+            else:
+                nc.scalar.copy(out=dst, in_=src)
+
+        def quant_w(g, c):
+            nc.vector.quantize_mx(
+                out=w_codes[:, g, c, :].bitcast(FP8X4), scales=w_scales[:, g, c, :], in_=tiles["w_grp", g, c][:]
+            )
+
+        def multiply(u, t, c):
+            g, m0, width = UNITS[u]
+            if c == 0:
+                tiles["acc", u, t] = psum.tile([P, width], F32, name="acc", tag="acc")
+            feats = slice(t * P, (t + 1) * P)
+            mols = slice(m0, m0 + width)
+            nc.tensor.matmul_mx(
+                out=tiles["acc", u, t][:],
+                lhsT=w_codes[:, g, c, feats].bitcast(FP8X4),
+                lhsT_scale=w_scales[:, g, c, feats],
+                rhs=x_codes[:, c, mols].bitcast(FP8X4),
+                rhs_scale=x_scales[:, c, mols],
+                start=(c == 0),
+                stop=(c == PASSES - 1),
+            )
+
+        def column(vec, u, t):
+            j = UNITS[u][0] * PACK + t
+            return vec[:, j : j + 1]
+
+        def to_turns(u):
+            y = work.tile([P, PACK, UNITS[u][2]], F32, name="y", bufs=4)
+            for t in range(PACK):
+                nc.scalar.activation(
+                    out=y[:, t, :], in_=tiles["acc", u, t][:], func=ACT.Identity,
+                    bias=column(shift, u, t), scale=column(rate, u, t),
+                )
+            tiles["y", u] = y
+
+        def whole_turns(u):
+            whole = work.tile([P, PACK, UNITS[u][2]], I32, name="whole", bufs=2)
+            nc.vector.tensor_copy(out=whole[:], in_=tiles["y", u][:])
+            tiles["whole", u] = whole
+
+        def rest_turns(u):
+            y = tiles["y", u]
+            nc.vector.tensor_tensor(out=y[:], in0=y[:], in1=tiles["whole", u][:], op=ALU.subtract)
+
+        def cosine(u):
+            y = tiles["y", u]
+            nc.scalar.activation(out=y[:], in_=y[:], func=ACT.Sin, scale=TWO_PI)
+
+        def scale(u):
+            y = tiles["y", u]
+            for t in range(PACK):
+                nc.vector.tensor_scalar(
+                    out=y[:, t, :], in0=y[:, t, :], scalar1=column(gain, u, t), scalar2=None, op0=ALU.mult
+                )
+
+        def turn_y(u, b):
+            bank = psum.tile([P, PACK, P], F32, name="turned", tag="turned")
+            for t in range(PACK):
+                nc.tensor.transpose(bank[:, t, :], tiles["y", u][:, t, b * P : (b + 1) * P], ident[:])
+            tiles["y_bank", u, b] = bank
+
+        def fetch_y(u, b, engine):
+            rows = work.tile([P, P, PACK], F32, name="y_rows", bufs=8)
+            src = tiles["y_bank", u, b][:].rearrange("m t p -> m p t")
+            if engine == "vector":
+                nc.vector.tensor_copy(out=rows[:], in_=src)
+            else:
+                nc.scalar.copy(out=rows[:], in_=src)
+            g, m0, width = UNITS[u]
+            nc.sync.dma_start(
+                out=out_0[m0 + b * P : m0 + (b + 1) * P, g * SPAN : (g + 1) * SPAN],
+                in_=rows[:].rearrange("m p t -> m (p t)"),
+            )
+
+        def group_y(u):
+            grp = work.tile([P, UNITS[u][2] * PACK], BF16, name="y_grp", bufs=2, align_bytes=64)
+            nc.vector.tensor_copy(
+                out=grp[:].rearrange("p (c i t) -> p c t i", i=4, t=PACK),
+                in_=tiles["y", u][:].rearrange("p t (c i) -> p c t i", i=4),
+            )
+            tiles["y_grp", u] = grp
+
+        def quant_y(u):
+            g, m0, width = UNITS[u]
+            mols = slice(m0, m0 + width)
+            codes = work.tile([P, width], U32, name="y_codes", bufs=3, align_bytes=64)
+            nc.vector.quantize_mx(out=codes[:].bitcast(FP8X4), scales=y_scales[:, g, mols], in_=tiles["y_grp", u][:])
+            dst = out_1[g].rearrange("p m t -> p (m t)").bitcast(I32)
+            nc.sync.dma_start(out=dst[:, mols], in_=codes[:].bitcast(I32))
+
+        def store_scales(g0, g1, queue):
+            for q in range(4):
+                queue.dma_start(
+                    out=out_2[g0:g1, 4 * q : 4 * q + 4, :].rearrange("g r m -> r g m").bitcast(I32),
+                    in_=y_scales[32 * q : 32 * q + 4, g0:g1, :].bitcast(I32),
+                )
+
+        for c in range(PASSES):
+            load_x(0, c)
+            load_w(0, c)
+        inv_raw = load_vector(inv_length, "inv_raw")
+        phase_raw = load_vector(phase, "phase_raw")
+        gain = load_vector(amp, "gain")
+        for c in range(PASSES):
+            load_x(1, c)
+        for g in range(1, GROUPS):
+            for c in range(PASSES):
+                load_w(g, c)
+
+        ident = keep.tile([P, P], F32, name="ident")
+        make_identity(nc, ident[:])
+        warm = keep.tile([P, 1], F32, name="warm")
+        nc.scalar.activation(out=warm[:], in_=ident[:, 0:1], func=ACT.Sin)
+
+        rate = keep.tile([P, GROUPS * PACK], F32, name="rate")
+        shift = keep.tile([P, GROUPS * PACK], F32, name="shift")
+
+        nc.vector.tensor_scalar(out=rate[:], in0=inv_raw, scalar1=1.0 / TWO_PI, scalar2=None, op0=ALU.mult)
+        nc.vector.tensor_scalar(
+            out=shift[:], in0=phase_raw, scalar1=1.0 / TWO_PI, scalar2=0.25, op0=ALU.mult, op1=ALU.add
+        )
+        for c in range(PASSES):
+            prepare_x(0, c)
+            group_w(0, c, "vector", 0, HEAD_SPLIT[c])
+            group_w(0, c, "scalar", HEAD_SPLIT[c], P)
+            quant_x(0, c)
+            quant_w(0, c)
+            for t in range(PACK):
+                multiply(0, t, c)
+        for c in range(PASSES):
+            prepare_x(1, c)
+            quant_x(1, c)
+
+        last = len(UNITS) - 1
+        for s in range(last + 3):
+            if s <= last:
+                to_turns(s)
+            if 1 <= s <= last + 1:
+                cosine(s - 1)
+            if s <= last:
+                whole_turns(s)
+            if s >= 2:
+                quant_y(s - 2)
+            if s <= last:
+                rest_turns(s)
+            for g, c, split in W_STEP.get(s, []):
+                group_w(g, c, "vector", 0, split)
+                group_w(g, c, "scalar", split, P)
+                quant_w(g, c)
+            if s < last:
+                for t in range(PACK):
+                    for c in range(PASSES):
+                        multiply(s + 1, t, c)
+            if 1 <= s <= last + 1:
+                scale(s - 1)
+                for b in range(UNITS[s - 1][2] // P):
+                    turn_y(s - 1, b)
+                    fetch_y(s - 1, b, "scalar")
+                group_y(s - 1)
+            if s == last:
+                store_scales(0, GROUPS - 1, nc.sync)
+        store_scales(GROUPS - 1, GROUPS, nc.scalar)

@@ -21,12 +21,16 @@ PACK = 4
 SPAN = P * PACK
 PASSES = K // SPAN
 GROUPS = N // SPAN
-HALVES = M // SPAN
-UNITS = [(g, h * SPAN, SPAN) for g in range(GROUPS) for h in range(HALVES)][:-1] + [(3, 512, 256), (3, 768, 128), (3, 896, 128)]
-W_STEP = {0: [(1, 0, 88)], 1: [(1, 1, 88), (1, 2, 88)], 2: [(2, 0, 88)], 3: [(2, 1, 88), (2, 2, 88)], 4: [(3, 0, 88)],
-          5: [(3, 1, 88), (3, 2, 88)]}
+QUARTER = M // 4
+UNITS = [(0, 0, 256), (0, 256, 256), (1, 0, 512), (0, 512, 512), (1, 512, 512), (2, 0, 512), (2, 512, 512),
+         (3, 0, 512), (3, 512, 256), (3, 768, 256)]
+ACC_BANKS = 3
+X_STEP = {-1: [(1, 0, "scalar"), (1, 1, "scalar")], 0: [(1, 2, "scalar")], 2: [(2, 0, "scalar")],
+          3: [(2, 1, "scalar"), (2, 2, "scalar"), (3, 0, "scalar")], 4: [(3, 1, "scalar"), (3, 2, "scalar")]}
+W_STEP = {0: (1, 0, 72), 1: (1, 1, 72), 2: (1, 2, 80), 6: (2, 0, 84), 7: (2, 1, 84), 8: (2, 2, 84),
+          10: (3, 0, 84), 11: (3, 1, 84), 12: (3, 2, 84)}
 TWO_PI = 2.0 * math.pi
-HEAD_SPLIT = (72, 72, 84)
+HEAD_SPLIT = (76, 76, 84)
 
 
 def tile_multiscale_random_cosine_features_g1_kernel(tc, x, w, inv_length, phase, amp, out_0, out_1, out_2):
@@ -44,11 +48,11 @@ def tile_multiscale_random_cosine_features_g1_kernel(tc, x, w, inv_length, phase
         w_scales = keep.tile([P, GROUPS, PASSES, SPAN], U8, name="w_scales", align_bytes=64)
         y_scales = keep.tile([P, GROUPS, M], U8, name="y_scales", align_bytes=64)
 
-        def load_x(h, c):
-            raw = keep.tile([P, PACK, SPAN], BF16, name="x_raw_%d_%d" % (h, c))
-            src = x[h * SPAN : (h + 1) * SPAN, c * SPAN : (c + 1) * SPAN]
+        def load_x(q, c):
+            raw = keep.tile([P, 2, SPAN], BF16, name="x_raw_%d_%d" % (q, c))
+            src = x[q * QUARTER : (q + 1) * QUARTER, c * SPAN : (c + 1) * SPAN]
             nc.sync.dma_start(out=raw[:], in_=src.rearrange("(i p) k -> p i k", p=P))
-            tiles["x_raw", h, c] = raw
+            tiles["x_raw", q, c] = raw
 
         def load_w(g, c):
             raw = keep.tile([P, PACK, SPAN], BF16, name="w_raw_%d_%d" % (g, c))
@@ -58,32 +62,36 @@ def tile_multiscale_random_cosine_features_g1_kernel(tc, x, w, inv_length, phase
 
         def load_vector(vec, name):
             raw = keep.tile([P, GROUPS, PACK], BF16, name=name)
-            nc.scalar.dma_start(out=raw[:], in_=vec.rearrange("(g p t) -> p g t", p=P, t=PACK))
+            nc.sync.dma_start(out=raw[:], in_=vec.rearrange("(g p t) -> p g t", p=P, t=PACK))
             return raw[:].rearrange("p g t -> p (g t)")
 
-        def prepare_x(h, c):
-            words = tiles["x_raw", h, c][:].bitcast(F32)
-            grp = work.tile([P, SPAN * PACK], BF16, name="x_grp", bufs=3, align_bytes=64)
-            for pair in range(2):
-                bank = psum.tile([P, 2, 2, P], F32, name="turned", tag="turned")
-                for i in range(2):
-                    for u in range(2):
-                        nc.tensor.transpose(bank[:, i, u, :], words[:, 2 * pair + i, u : 2 * P : 2], ident[:])
-                dst = grp[:].bitcast(F32)[:, pair * SPAN : (pair + 1) * SPAN]
-                nc.scalar.copy(
-                    out=dst.rearrange("p (i r u) -> p i r u", i=2, u=2), in_=bank[:].rearrange("p i u r -> p i r u")
-                )
-            tiles["x_grp", h, c] = grp
+        def turn_x(q, c):
+            bank = psum.tile([P, 2, 2, P], F32, name="turned", tag="turned", bufs=8 - ACC_BANKS)
+            words = tiles["x_raw", q, c][:].bitcast(F32)
+            for i in range(2):
+                for u in range(2):
+                    nc.tensor.transpose(bank[:, i, u, :], words[:, i, u : 2 * P : 2], ident[:])
+            tiles["x_bank", q, c] = bank
 
-        def quant_x(h, c):
-            cols = slice(h * SPAN, (h + 1) * SPAN)
+        def group_x(q, c, engine):
+            grp = work.tile([P, QUARTER * PACK], BF16, name="x_grp", bufs=6, align_bytes=64)
+            dst = grp[:].bitcast(F32).rearrange("p (i r u) -> p i r u", i=2, u=2)
+            src = tiles["x_bank", q, c][:].rearrange("p i u r -> p i r u")
+            if engine == "vector":
+                nc.vector.tensor_copy(out=dst, in_=src)
+            else:
+                nc.scalar.copy(out=dst, in_=src)
+            tiles["x_grp", q, c] = grp
+
+        def quant_x(q, c):
+            cols = slice(q * QUARTER, (q + 1) * QUARTER)
             nc.vector.quantize_mx(
-                out=x_codes[:, c, cols].bitcast(FP8X4), scales=x_scales[:, c, cols], in_=tiles["x_grp", h, c][:]
+                out=x_codes[:, c, cols].bitcast(FP8X4), scales=x_scales[:, c, cols], in_=tiles["x_grp", q, c][:]
             )
 
         def group_w(g, c, engine, m0, m1):
             if ("w_grp", g, c) not in tiles:
-                tiles["w_grp", g, c] = work.tile([P, SPAN * PACK], BF16, name="w_grp", bufs=4, align_bytes=64)
+                tiles["w_grp", g, c] = work.tile([P, SPAN * PACK], BF16, name="w_grp", bufs=3, align_bytes=64)
             dst = tiles["w_grp", g, c][:].rearrange("p (t m j) -> p m t j", t=PACK, j=PACK)[:, m0:m1]
             src = tiles["w_raw", g, c][:].rearrange("p j (m t) -> p m t j", t=PACK)[:, m0:m1]
             if engine == "vector":
@@ -99,7 +107,7 @@ def tile_multiscale_random_cosine_features_g1_kernel(tc, x, w, inv_length, phase
         def multiply(u, t, c):
             g, m0, width = UNITS[u]
             if c == 0:
-                tiles["acc", u, t] = psum.tile([P, width], F32, name="acc", tag="acc")
+                tiles["acc", u, t] = psum.tile([P, width], F32, name="acc", tag="acc", bufs=ACC_BANKS)
             feats = slice(t * P, (t + 1) * P)
             mols = slice(m0, m0 + width)
             nc.tensor.matmul_mx(
@@ -116,43 +124,50 @@ def tile_multiscale_random_cosine_features_g1_kernel(tc, x, w, inv_length, phase
             j = UNITS[u][0] * PACK + t
             return vec[:, j : j + 1]
 
-        def to_turns(u):
-            y = work.tile([P, PACK, UNITS[u][2]], F32, name="y", bufs=4)
-            for t in range(PACK):
-                nc.scalar.activation(
-                    out=y[:, t, :], in_=tiles["acc", u, t][:], func=ACT.Identity,
-                    bias=column(shift, u, t), scale=column(rate, u, t),
-                )
-            tiles["y", u] = y
+        def to_turns(s, i):
+            u, pair = divmod(s, 2)
+            if i == 0:
+                tiles["turns", s] = work.tile([P, 2, UNITS[u][2]], F32, name="turns", bufs=3)
+            t = 2 * pair + i
+            nc.scalar.activation(
+                out=tiles["turns", s][:, i, :], in_=tiles["acc", u, t][:], func=ACT.Identity,
+                bias=column(shift, u, t), scale=column(rate, u, t),
+            )
 
-        def whole_turns(u):
-            whole = work.tile([P, PACK, UNITS[u][2]], I32, name="whole", bufs=2)
-            nc.vector.tensor_copy(out=whole[:], in_=tiles["y", u][:])
-            tiles["whole", u] = whole
+        def whole_turns(s):
+            whole = work.tile([P, 2, UNITS[s // 2][2]], I32, name="whole", bufs=2)
+            nc.vector.tensor_copy(out=whole[:], in_=tiles["turns", s][:])
+            tiles["whole", s] = whole
 
-        def rest_turns(u):
-            y = tiles["y", u]
-            nc.vector.tensor_tensor(out=y[:], in0=y[:], in1=tiles["whole", u][:], op=ALU.subtract)
+        def rest_turns(s):
+            rest = work.tile([P, 2, UNITS[s // 2][2]], F32, name="rest", bufs=3)
+            nc.vector.tensor_tensor(out=rest[:], in0=tiles["turns", s][:], in1=tiles["whole", s][:], op=ALU.subtract)
+            tiles["rest", s] = rest
 
-        def cosine(u):
-            y = tiles["y", u]
-            nc.scalar.activation(out=y[:], in_=y[:], func=ACT.Sin, scale=TWO_PI)
+        def cosine(s):
+            wave = work.tile([P, 2, UNITS[s // 2][2]], F32, name="wave", bufs=3)
+            nc.scalar.activation(out=wave[:], in_=tiles["rest", s][:], func=ACT.Sin, scale=TWO_PI)
+            tiles["wave", s] = wave
 
-        def scale(u):
-            y = tiles["y", u]
-            for t in range(PACK):
+        def scale(s):
+            u, pair = divmod(s, 2)
+            if pair == 0:
+                tiles["y", u] = work.tile([P, PACK, UNITS[u][2]], F32, name="y", bufs=2)
+            for i in range(2):
+                t = 2 * pair + i
                 nc.vector.tensor_scalar(
-                    out=y[:, t, :], in0=y[:, t, :], scalar1=column(gain, u, t), scalar2=None, op0=ALU.mult
+                    out=tiles["y", u][:, t, :], in0=tiles["wave", s][:, i, :], scalar1=column(gain, u, t),
+                    scalar2=None, op0=ALU.mult,
                 )
 
         def turn_y(u, b):
-            bank = psum.tile([P, PACK, P], F32, name="turned", tag="turned")
+            bank = psum.tile([P, PACK, P], F32, name="turned", tag="turned", bufs=8 - ACC_BANKS)
             for t in range(PACK):
                 nc.tensor.transpose(bank[:, t, :], tiles["y", u][:, t, b * P : (b + 1) * P], ident[:])
             tiles["y_bank", u, b] = bank
 
         def fetch_y(u, b, engine):
-            rows = work.tile([P, P, PACK], F32, name="y_rows", bufs=8)
+            rows = work.tile([P, P, PACK], F32, name="y_rows", bufs=6)
             src = tiles["y_bank", u, b][:].rearrange("m t p -> m p t")
             if engine == "vector":
                 nc.vector.tensor_copy(out=rows[:], in_=src)
@@ -164,21 +179,28 @@ def tile_multiscale_random_cosine_features_g1_kernel(tc, x, w, inv_length, phase
                 in_=rows[:].rearrange("m p t -> m (p t)"),
             )
 
-        def group_y(u):
-            grp = work.tile([P, UNITS[u][2] * PACK], BF16, name="y_grp", bufs=2, align_bytes=64)
+        def group_y(u, half):
+            width = UNITS[u][2] // 2
+            grp = work.tile([P, width * PACK], BF16, name="y_grp", bufs=3, align_bytes=64)
             nc.vector.tensor_copy(
                 out=grp[:].rearrange("p (c i t) -> p c t i", i=4, t=PACK),
-                in_=tiles["y", u][:].rearrange("p t (c i) -> p c t i", i=4),
+                in_=tiles["y", u][:, :, half * width : (half + 1) * width].rearrange("p t (c i) -> p c t i", i=4),
             )
-            tiles["y_grp", u] = grp
+            tiles["y_grp", u, half] = grp
 
-        def quant_y(u):
+        def quant_y(u, half):
             g, m0, width = UNITS[u]
-            mols = slice(m0, m0 + width)
-            codes = work.tile([P, width], U32, name="y_codes", bufs=3, align_bytes=64)
-            nc.vector.quantize_mx(out=codes[:].bitcast(FP8X4), scales=y_scales[:, g, mols], in_=tiles["y_grp", u][:])
-            dst = out_1[g].rearrange("p m t -> p (m t)").bitcast(I32)
-            nc.sync.dma_start(out=dst[:, mols], in_=codes[:].bitcast(I32))
+            if half == 0:
+                tiles["y_codes", u] = work.tile([P, width], U32, name="y_codes", bufs=3, align_bytes=64)
+            codes = tiles["y_codes", u]
+            lo, hi = half * width // 2, (half + 1) * width // 2
+            nc.vector.quantize_mx(
+                out=codes[:, lo:hi].bitcast(FP8X4), scales=y_scales[:, g, m0 + lo : m0 + hi],
+                in_=tiles["y_grp", u, half][:],
+            )
+            if half == 1:
+                dst = out_1[g].rearrange("p m t -> p (m t)").bitcast(I32)
+                nc.sync.dma_start(out=dst[:, m0 : m0 + width], in_=codes[:].bitcast(I32))
 
         def store_scales(g0, g1, queue):
             for q in range(4):
@@ -193,11 +215,9 @@ def tile_multiscale_random_cosine_features_g1_kernel(tc, x, w, inv_length, phase
         inv_raw = load_vector(inv_length, "inv_raw")
         phase_raw = load_vector(phase, "phase_raw")
         gain = load_vector(amp, "gain")
-        for c in range(PASSES):
-            load_x(1, c)
-        for g in range(1, GROUPS):
+        for load, part in ((load_x, 1), (load_w, 1), (load_x, 2), (load_x, 3), (load_w, 2), (load_w, 3)):
             for c in range(PASSES):
-                load_w(g, c)
+                load(part, c)
 
         ident = keep.tile([P, P], F32, name="ident")
         make_identity(nc, ident[:])
@@ -207,48 +227,73 @@ def tile_multiscale_random_cosine_features_g1_kernel(tc, x, w, inv_length, phase
         rate = keep.tile([P, GROUPS * PACK], F32, name="rate")
         shift = keep.tile([P, GROUPS * PACK], F32, name="shift")
 
-        nc.vector.tensor_scalar(out=rate[:], in0=inv_raw, scalar1=1.0 / TWO_PI, scalar2=None, op0=ALU.mult)
-        nc.vector.tensor_scalar(
-            out=shift[:], in0=phase_raw, scalar1=1.0 / TWO_PI, scalar2=0.25, op0=ALU.mult, op1=ALU.add
-        )
         for c in range(PASSES):
-            prepare_x(0, c)
+            turn_x(0, c)
+            group_x(0, c, "scalar")
             group_w(0, c, "vector", 0, HEAD_SPLIT[c])
             group_w(0, c, "scalar", HEAD_SPLIT[c], P)
+            if c == 1:
+                nc.vector.tensor_scalar(out=rate[:], in0=inv_raw, scalar1=1.0 / TWO_PI, scalar2=None, op0=ALU.mult)
+                nc.vector.tensor_scalar(
+                    out=shift[:], in0=phase_raw, scalar1=1.0 / TWO_PI, scalar2=0.25, op0=ALU.mult, op1=ALU.add
+                )
             quant_x(0, c)
             quant_w(0, c)
-            for t in range(PACK):
-                multiply(0, t, c)
         for c in range(PASSES):
-            prepare_x(1, c)
-            quant_x(1, c)
+            if c == PASSES - 1:
+                turn_x(1, 0)
+            for t in range(ACC_BANKS):
+                multiply(0, t, c)
+        turn_x(1, 1)
+        for q, c, engine in X_STEP[-1]:
+            group_x(q, c, engine)
+            quant_x(q, c)
 
-        last = len(UNITS) - 1
-        for s in range(last + 3):
-            if s <= last:
-                to_turns(s)
-            if 1 <= s <= last + 1:
-                cosine(s - 1)
-            if s <= last:
-                whole_turns(s)
-            if s >= 2:
-                quant_y(s - 2)
-            if s <= last:
-                rest_turns(s)
-            for g, c, split in W_STEP.get(s, []):
-                group_w(g, c, "vector", 0, split)
-                group_w(g, c, "scalar", split, P)
-                quant_w(g, c)
-            if s < last:
-                for t in range(PACK):
+        steps = 2 * len(UNITS)
+        for s in range(steps + 5):
+            done, half = divmod(s - 5, 2)
+            x_now = X_STEP.get(s, [])
+            for i in range(2):
+                if s < steps:
+                    to_turns(s, i)
+                if i == 0:
+                    for q, c, engine in x_now:
+                        turn_x(q, c)
+                    if 2 <= s < steps + 2:
+                        cosine(s - 2)
+                    if s >= 5 and s % 2 == 1:
+                        for b in range(UNITS[done][2] // P):
+                            turn_y(done, b)
+            if 1 <= s <= steps:
+                whole_turns(s - 1)
+            if 3 <= s < steps + 3:
+                scale(s - 3)
+            if 1 <= s <= steps:
+                rest_turns(s - 1)
+            for q, c, engine in x_now:
+                group_x(q, c, engine)
+            if s in W_STEP:
+                group_w(W_STEP[s][0], W_STEP[s][1], "scalar", W_STEP[s][2], P)
+            if 5 <= s:
+                per_step = UNITS[done][2] // P // 2
+                for b in range(half * per_step, (half + 1) * per_step):
+                    fetch_y(done, b, "scalar")
+            if 5 <= s < steps + 4:
+                quant_y((s - 5) // 2, (s - 5) % 2)
+            if s in W_STEP:
+                group_w(W_STEP[s][0], W_STEP[s][1], "vector", 0, W_STEP[s][2])
+            if 4 <= s < steps + 4:
+                group_y((s - 4) // 2, (s - 4) % 2)
+            for q, c, engine in x_now:
+                quant_x(q, c)
+            if s in W_STEP:
+                quant_w(W_STEP[s][0], W_STEP[s][1])
+            for i in range(2):
+                u, t = divmod(2 * s + i + ACC_BANKS, PACK)
+                if u < len(UNITS):
                     for c in range(PASSES):
-                        multiply(s + 1, t, c)
-            if 1 <= s <= last + 1:
-                scale(s - 1)
-                for b in range(UNITS[s - 1][2] // P):
-                    turn_y(s - 1, b)
-                    fetch_y(s - 1, b, "scalar")
-                group_y(s - 1)
-            if s == last:
+                        multiply(u, t, c)
+            if s == steps + 1:
                 store_scales(0, GROUPS - 1, nc.sync)
+        quant_y(len(UNITS) - 1, 1)
         store_scales(GROUPS - 1, GROUPS, nc.scalar)

@@ -24,11 +24,11 @@ GROUPS = N // SPAN
 QUARTER = M // 4
 UNITS = [(0, 0, 256), (0, 256, 256), (1, 0, 512), (0, 512, 512), (1, 512, 512), (2, 0, 512), (2, 512, 512),
          (3, 0, 512), (3, 512, 256), (3, 768, 256)]
+STEPS = [(u, ts) for u, unit in enumerate(UNITS) for ts in (((0, 1), (2, 3)) if unit[2] == SPAN else ((0, 1, 2, 3),))]
 ACC_BANKS = 3
-X_STEP = {-1: [(1, 0, "scalar"), (1, 1, "scalar")], 0: [(1, 2, "scalar")], 2: [(2, 0, "scalar")],
-          3: [(2, 1, "scalar"), (2, 2, "scalar"), (3, 0, "scalar")], 4: [(3, 1, "scalar"), (3, 2, "scalar")]}
-W_STEP = {0: (1, 0, 72), 1: (1, 1, 72), 2: (1, 2, 80), 6: (2, 0, 84), 7: (2, 1, 84), 8: (2, 2, 84),
-          10: (3, 0, 84), 11: (3, 1, 84), 12: (3, 2, 84)}
+X_STEP = {1: [(2, 0), (2, 1), (2, 2)], 2: [(3, 0), (3, 1), (3, 2)]}
+W_STEP = {0: [(1, 0, 72), (1, 1, 72)], 1: [(1, 2, 80)], 4: [(2, 0, 88)], 5: [(2, 1, 88)], 6: [(2, 2, 88)],
+          8: [(3, 0, 88)], 9: [(3, 1, 88)], 10: [(3, 2, 88)]}
 TWO_PI = 2.0 * math.pi
 HEAD_SPLIT = (76, 76, 84)
 
@@ -60,11 +60,6 @@ def tile_multiscale_random_cosine_features_g1_kernel(tc, x, w, inv_length, phase
             nc.sync.dma_start(out=raw[:], in_=src.rearrange("(p j) n -> p j n", j=PACK))
             tiles["w_raw", g, c] = raw
 
-        def load_vector(vec, name):
-            raw = keep.tile([P, GROUPS, PACK], BF16, name=name)
-            nc.sync.dma_start(out=raw[:], in_=vec.rearrange("(g p t) -> p g t", p=P, t=PACK))
-            return raw[:].rearrange("p g t -> p (g t)")
-
         def turn_x(q, c):
             bank = psum.tile([P, 2, 2, P], F32, name="turned", tag="turned", bufs=8 - ACC_BANKS)
             words = tiles["x_raw", q, c][:].bitcast(F32)
@@ -73,14 +68,12 @@ def tile_multiscale_random_cosine_features_g1_kernel(tc, x, w, inv_length, phase
                     nc.tensor.transpose(bank[:, i, u, :], words[:, i, u : 2 * P : 2], ident[:])
             tiles["x_bank", q, c] = bank
 
-        def group_x(q, c, engine):
+        def group_x(q, c):
             grp = work.tile([P, QUARTER * PACK], BF16, name="x_grp", bufs=6, align_bytes=64)
-            dst = grp[:].bitcast(F32).rearrange("p (i r u) -> p i r u", i=2, u=2)
-            src = tiles["x_bank", q, c][:].rearrange("p i u r -> p i r u")
-            if engine == "vector":
-                nc.vector.tensor_copy(out=dst, in_=src)
-            else:
-                nc.scalar.copy(out=dst, in_=src)
+            nc.scalar.copy(
+                out=grp[:].bitcast(F32).rearrange("p (i r u) -> p i r u", i=2, u=2),
+                in_=tiles["x_bank", q, c][:].rearrange("p i u r -> p i r u"),
+            )
             tiles["x_grp", q, c] = grp
 
         def quant_x(q, c):
@@ -92,8 +85,8 @@ def tile_multiscale_random_cosine_features_g1_kernel(tc, x, w, inv_length, phase
         def group_w(g, c, engine, m0, m1):
             if ("w_grp", g, c) not in tiles:
                 tiles["w_grp", g, c] = work.tile([P, SPAN * PACK], BF16, name="w_grp", bufs=3, align_bytes=64)
-            dst = tiles["w_grp", g, c][:].rearrange("p (t m j) -> p m t j", t=PACK, j=PACK)[:, m0:m1]
-            src = tiles["w_raw", g, c][:].rearrange("p j (m t) -> p m t j", t=PACK)[:, m0:m1]
+            dst = tiles["w_grp", g, c][:].rearrange("p (t a b j) -> p a j b t", t=PACK, j=PACK, b=2)[:, m0 // 2 : m1 // 2]
+            src = tiles["w_raw", g, c][:].rearrange("p j (a b t) -> p a j b t", t=PACK, b=2)[:, m0 // 2 : m1 // 2]
             if engine == "vector":
                 nc.vector.tensor_copy(out=dst, in_=src)
             else:
@@ -121,40 +114,38 @@ def tile_multiscale_random_cosine_features_g1_kernel(tc, x, w, inv_length, phase
             )
 
         def column(vec, u, t):
-            j = UNITS[u][0] * PACK + t
-            return vec[:, j : j + 1]
+            g = UNITS[u][0]
+            return vec[:, t // 2, t % 2, g : g + 1]
 
         def to_turns(s, i):
-            u, pair = divmod(s, 2)
+            u, ts = STEPS[s]
             if i == 0:
-                tiles["turns", s] = work.tile([P, 2, UNITS[u][2]], F32, name="turns", bufs=3)
-            t = 2 * pair + i
+                tiles["turns", s] = work.tile([P, len(ts), UNITS[u][2]], F32, name="turns", bufs=3)
             nc.scalar.activation(
-                out=tiles["turns", s][:, i, :], in_=tiles["acc", u, t][:], func=ACT.Identity,
-                bias=column(shift, u, t), scale=column(rate, u, t),
+                out=tiles["turns", s][:, i, :], in_=tiles["acc", u, ts[i]][:], func=ACT.Identity,
+                bias=column(shift, u, ts[i]), scale=column(rate, u, ts[i]),
             )
 
         def whole_turns(s):
-            whole = work.tile([P, 2, UNITS[s // 2][2]], I32, name="whole", bufs=2)
+            whole = work.tile(tiles["turns", s].shape, I32, name="whole", bufs=2)
             nc.vector.tensor_copy(out=whole[:], in_=tiles["turns", s][:])
             tiles["whole", s] = whole
 
         def rest_turns(s):
-            rest = work.tile([P, 2, UNITS[s // 2][2]], F32, name="rest", bufs=3)
+            rest = work.tile(tiles["turns", s].shape, F32, name="rest", bufs=3)
             nc.vector.tensor_tensor(out=rest[:], in0=tiles["turns", s][:], in1=tiles["whole", s][:], op=ALU.subtract)
             tiles["rest", s] = rest
 
         def cosine(s):
-            wave = work.tile([P, 2, UNITS[s // 2][2]], F32, name="wave", bufs=3)
+            wave = work.tile(tiles["rest", s].shape, F32, name="wave", bufs=3)
             nc.scalar.activation(out=wave[:], in_=tiles["rest", s][:], func=ACT.Sin, scale=TWO_PI)
             tiles["wave", s] = wave
 
         def scale(s):
-            u, pair = divmod(s, 2)
-            if pair == 0:
+            u, ts = STEPS[s]
+            if ts[0] == 0:
                 tiles["y", u] = work.tile([P, PACK, UNITS[u][2]], F32, name="y", bufs=2)
-            for i in range(2):
-                t = 2 * pair + i
+            for i, t in enumerate(ts):
                 nc.vector.tensor_scalar(
                     out=tiles["y", u][:, t, :], in0=tiles["wave", s][:, i, :], scalar1=column(gain, u, t),
                     scalar2=None, op0=ALU.mult,
@@ -166,41 +157,30 @@ def tile_multiscale_random_cosine_features_g1_kernel(tc, x, w, inv_length, phase
                 nc.tensor.transpose(bank[:, t, :], tiles["y", u][:, t, b * P : (b + 1) * P], ident[:])
             tiles["y_bank", u, b] = bank
 
-        def fetch_y(u, b, engine):
-            rows = work.tile([P, P, PACK], F32, name="y_rows", bufs=6)
-            src = tiles["y_bank", u, b][:].rearrange("m t p -> m p t")
-            if engine == "vector":
-                nc.vector.tensor_copy(out=rows[:], in_=src)
-            else:
-                nc.scalar.copy(out=rows[:], in_=src)
+        def fetch_y(u, b):
+            rows = work.tile([P, P, PACK], F32, name="y_rows", bufs=8)
+            nc.scalar.copy(out=rows[:], in_=tiles["y_bank", u, b][:].rearrange("m t p -> m p t"))
             g, m0, width = UNITS[u]
             nc.sync.dma_start(
                 out=out_0[m0 + b * P : m0 + (b + 1) * P, g * SPAN : (g + 1) * SPAN],
                 in_=rows[:].rearrange("m p t -> m (p t)"),
             )
 
-        def group_y(u, half):
-            width = UNITS[u][2] // 2
-            grp = work.tile([P, width * PACK], BF16, name="y_grp", bufs=3, align_bytes=64)
+        def group_y(u):
+            grp = work.tile([P, UNITS[u][2] * PACK], BF16, name="y_grp", bufs=2, align_bytes=64)
             nc.vector.tensor_copy(
                 out=grp[:].rearrange("p (c i t) -> p c t i", i=4, t=PACK),
-                in_=tiles["y", u][:, :, half * width : (half + 1) * width].rearrange("p t (c i) -> p c t i", i=4),
+                in_=tiles["y", u][:].rearrange("p t (c i) -> p c t i", i=4),
             )
-            tiles["y_grp", u, half] = grp
+            tiles["y_grp", u] = grp
 
-        def quant_y(u, half):
+        def quant_y(u):
             g, m0, width = UNITS[u]
-            if half == 0:
-                tiles["y_codes", u] = work.tile([P, width], U32, name="y_codes", bufs=3, align_bytes=64)
-            codes = tiles["y_codes", u]
-            lo, hi = half * width // 2, (half + 1) * width // 2
-            nc.vector.quantize_mx(
-                out=codes[:, lo:hi].bitcast(FP8X4), scales=y_scales[:, g, m0 + lo : m0 + hi],
-                in_=tiles["y_grp", u, half][:],
-            )
-            if half == 1:
-                dst = out_1[g].rearrange("p m t -> p (m t)").bitcast(I32)
-                nc.sync.dma_start(out=dst[:, m0 : m0 + width], in_=codes[:].bitcast(I32))
+            mols = slice(m0, m0 + width)
+            codes = work.tile([P, width], U32, name="y_codes", bufs=3, align_bytes=64)
+            nc.vector.quantize_mx(out=codes[:].bitcast(FP8X4), scales=y_scales[:, g, mols], in_=tiles["y_grp", u][:])
+            dst = out_1[g].rearrange("p m t -> p (m t)").bitcast(I32)
+            nc.sync.dma_start(out=dst[:, mols], in_=codes[:].bitcast(I32))
 
         def store_scales(g0, g1, queue):
             for q in range(4):
@@ -209,12 +189,15 @@ def tile_multiscale_random_cosine_features_g1_kernel(tc, x, w, inv_length, phase
                     in_=y_scales[32 * q : 32 * q + 4, g0:g1, :].bitcast(I32),
                 )
 
+        vec_rows = keep.tile([P, SPAN], BF16, name="vec_rows")
+        nc.vector.memset(vec_rows[:], 0.0)
         for c in range(PASSES):
             load_x(0, c)
             load_w(0, c)
-        inv_raw = load_vector(inv_length, "inv_raw")
-        phase_raw = load_vector(phase, "phase_raw")
-        gain = load_vector(amp, "gain")
+            vec = (inv_length, phase, amp)[c]
+            nc.sync.dma_start(
+                out=vec_rows[c * GROUPS : (c + 1) * GROUPS, :], in_=vec.rearrange("(g n) -> g n", g=GROUPS)
+            )
         for load, part in ((load_x, 1), (load_w, 1), (load_x, 2), (load_x, 3), (load_w, 2), (load_w, 3)):
             for c in range(PASSES):
                 load(part, c)
@@ -224,76 +207,77 @@ def tile_multiscale_random_cosine_features_g1_kernel(tc, x, w, inv_length, phase
         warm = keep.tile([P, 1], F32, name="warm")
         nc.scalar.activation(out=warm[:], in_=ident[:, 0:1], func=ACT.Sin)
 
-        rate = keep.tile([P, GROUPS * PACK], F32, name="rate")
-        shift = keep.tile([P, GROUPS * PACK], F32, name="shift")
+        rate = keep.tile([P, 2, 2, GROUPS], F32, name="rate")
+        shift = keep.tile([P, 2, 2, GROUPS], F32, name="shift")
+        gain = keep.tile([P, 2, 2, GROUPS], F32, name="gain")
+
+        def spread_vectors():
+            bank = psum.tile([P, 2, P], F32, name="turned", tag="turned", bufs=8 - ACC_BANKS)
+            words = vec_rows[:].bitcast(F32)
+            for u in range(2):
+                nc.tensor.transpose(bank[:, u, :], words[:, u : 2 * P : 2], ident[:])
+            cols = bank[:].bitcast(BF16).rearrange("p u (r e) -> p u e r", e=2)
+            nc.vector.tensor_scalar(
+                out=rate[:], in0=cols[:, :, :, 0:GROUPS], scalar1=1.0 / TWO_PI, scalar2=None, op0=ALU.mult
+            )
+            nc.vector.tensor_scalar(
+                out=shift[:], in0=cols[:, :, :, GROUPS : 2 * GROUPS], scalar1=1.0 / TWO_PI, scalar2=0.25,
+                op0=ALU.mult, op1=ALU.add,
+            )
+            nc.vector.tensor_copy(out=gain[:], in_=cols[:, :, :, 2 * GROUPS : 3 * GROUPS])
 
         for c in range(PASSES):
             turn_x(0, c)
-            group_x(0, c, "scalar")
+            if c == PASSES - 1:
+                spread_vectors()
+            group_x(0, c)
             group_w(0, c, "vector", 0, HEAD_SPLIT[c])
             group_w(0, c, "scalar", HEAD_SPLIT[c], P)
-            if c == 1:
-                nc.vector.tensor_scalar(out=rate[:], in0=inv_raw, scalar1=1.0 / TWO_PI, scalar2=None, op0=ALU.mult)
-                nc.vector.tensor_scalar(
-                    out=shift[:], in0=phase_raw, scalar1=1.0 / TWO_PI, scalar2=0.25, op0=ALU.mult, op1=ALU.add
-                )
             quant_x(0, c)
             quant_w(0, c)
         for c in range(PASSES):
-            if c == PASSES - 1:
-                turn_x(1, 0)
             for t in range(ACC_BANKS):
                 multiply(0, t, c)
-        turn_x(1, 1)
-        for q, c, engine in X_STEP[-1]:
-            group_x(q, c, engine)
-            quant_x(q, c)
+        for c in range(PASSES):
+            turn_x(1, c)
+            group_x(1, c)
+            quant_x(1, c)
 
-        steps = 2 * len(UNITS)
+        order = [(u, t) for u in range(len(UNITS)) for t in range(PACK)]
+        steps = len(STEPS)
+        ends = {s: u for s, (u, ts) in enumerate(STEPS) if ts[-1] == PACK - 1}
         for s in range(steps + 5):
-            done, half = divmod(s - 5, 2)
-            x_now = X_STEP.get(s, [])
-            for i in range(2):
-                if s < steps:
+            if s - 4 in ends:
+                u = ends[s - 4]
+                for b in range(UNITS[u][2] // P):
+                    turn_y(u, b)
+                    fetch_y(u, b)
+                group_y(u)
+            for q, c in X_STEP.get(s, []):
+                turn_x(q, c)
+                group_x(q, c)
+                quant_x(q, c)
+            for g, c, split in W_STEP.get(s, []):
+                group_w(g, c, "vector", 0, split)
+                group_w(g, c, "scalar", split, P)
+                quant_w(g, c)
+            if s < steps:
+                for i, t in enumerate(STEPS[s][1]):
                     to_turns(s, i)
-                if i == 0:
-                    for q, c, engine in x_now:
-                        turn_x(q, c)
-                    if 2 <= s < steps + 2:
-                        cosine(s - 2)
-                    if s >= 5 and s % 2 == 1:
-                        for b in range(UNITS[done][2] // P):
-                            turn_y(done, b)
+                    ahead = STEPS[s][0] * PACK + t + ACC_BANKS
+                    if ahead < len(order):
+                        for c in range(PASSES):
+                            multiply(order[ahead][0], order[ahead][1], c)
+            if 2 <= s < steps + 2:
+                cosine(s - 2)
             if 1 <= s <= steps:
                 whole_turns(s - 1)
             if 3 <= s < steps + 3:
                 scale(s - 3)
             if 1 <= s <= steps:
                 rest_turns(s - 1)
-            for q, c, engine in x_now:
-                group_x(q, c, engine)
-            if s in W_STEP:
-                group_w(W_STEP[s][0], W_STEP[s][1], "scalar", W_STEP[s][2], P)
-            if 5 <= s:
-                per_step = UNITS[done][2] // P // 2
-                for b in range(half * per_step, (half + 1) * per_step):
-                    fetch_y(done, b, "scalar")
-            if 5 <= s < steps + 4:
-                quant_y((s - 5) // 2, (s - 5) % 2)
-            if s in W_STEP:
-                group_w(W_STEP[s][0], W_STEP[s][1], "vector", 0, W_STEP[s][2])
-            if 4 <= s < steps + 4:
-                group_y((s - 4) // 2, (s - 4) % 2)
-            for q, c, engine in x_now:
-                quant_x(q, c)
-            if s in W_STEP:
-                quant_w(W_STEP[s][0], W_STEP[s][1])
-            for i in range(2):
-                u, t = divmod(2 * s + i + ACC_BANKS, PACK)
-                if u < len(UNITS):
-                    for c in range(PASSES):
-                        multiply(u, t, c)
-            if s == steps + 1:
+            if s - 5 in ends:
+                quant_y(ends[s - 5])
+            if s == steps + 2:
                 store_scales(0, GROUPS - 1, nc.sync)
-        quant_y(len(UNITS) - 1, 1)
         store_scales(GROUPS - 1, GROUPS, nc.scalar)

import math
from contextlib import ExitStack

import concourse.mybir as mybir
from concourse.masks import make_identity

M, K, N = 1024, 1536, 2048
FLOPS = 2 * M * K * N

F32 = mybir.dt.float32
BF16 = mybir.dt.bfloat16
I32 = mybir.dt.int32
U32 = mybir.dt.uint32
U8 = mybir.dt.uint8
FP8X4 = mybir.dt.float8_e4m3fn_x4
ALU = mybir.AluOpType
ACT = mybir.ActivationFunctionType

P = 128
PACK = 4
SPAN = P * PACK
PASSES = K // SPAN
GROUPS = N // SPAN
QUARTER = M // 4
UNITS = [(0, 0, 256), (0, 256, 256), (1, 0, 512), (0, 512, 512), (1, 512, 512), (2, 0, 512), (2, 512, 512),
         (3, 0, 512), (3, 512, 256), (3, 768, 256)]
STEPS = [(u, ts) for u, unit in enumerate(UNITS) for ts in (((0, 1), (2, 3)) if unit[2] == SPAN else ((0, 1, 2, 3),))]
ACC_BANKS = 3
X_STEP = {1: [(2, 0), (2, 1), (2, 2)], 2: [(3, 0), (3, 1), (3, 2)]}
W_STEP = {0: [(1, 0, 72), (1, 1, 72)], 1: [(1, 2, 80)], 4: [(2, 0, 88)], 5: [(2, 1, 88)], 6: [(2, 2, 88)],
          8: [(3, 0, 88)], 9: [(3, 1, 88)], 10: [(3, 2, 88)]}
TWO_PI = 2.0 * math.pi
HEAD_SPLIT = (76, 76, 84)


def tile_multiscale_random_cosine_features_g1_kernel(tc, x, w, inv_length, phase, amp, out_0, out_1, out_2):
    nc = tc.nc
    with ExitStack() as ctx:
        keep = ctx.enter_context(tc.tile_pool(name="keep", bufs=1))
        work = ctx.enter_context(tc.tile_pool(name="work", bufs=2))
        psum = ctx.enter_context(tc.psum_pool(name="psum", bufs=4))

        tiles = {}

        x_codes = keep.tile([P, PASSES, M], U32, name="x_codes", align_bytes=64)
        x_scales = keep.tile([P, PASSES, M], U8, name="x_scales", align_bytes=64)
        w_codes = keep.tile([P, GROUPS, PASSES, SPAN], U32, name="w_codes", align_bytes=64)
        w_scales = keep.tile([P, GROUPS, PASSES, SPAN], U8, name="w_scales", align_bytes=64)
        y_scales = keep.tile([P, GROUPS, M], U8, name="y_scales", align_bytes=64)

        def load_x(q, c):
            raw = keep.tile([P, 2, SPAN], BF16, name="x_raw_%d_%d" % (q, c))
            src = x[q * QUARTER : (q + 1) * QUARTER, c * SPAN : (c + 1) * SPAN]
            nc.sync.dma_start(out=raw[:], in_=src.rearrange("(i p) k -> p i k", p=P))
            tiles["x_raw", q, c] = raw

        def load_w(g, c):
            raw = keep.tile([P, PACK, SPAN], BF16, name="w_raw_%d_%d" % (g, c))
            src = w[c * SPAN : (c + 1) * SPAN, g * SPAN : (g + 1) * SPAN]
            nc.sync.dma_start(out=raw[:], in_=src.rearrange("(p j) n -> p j n", j=PACK))
            tiles["w_raw", g, c] = raw

        def turn_x(q, c):
            bank = psum.tile([P, 2, 2, P], F32, name="turned", tag="turned", bufs=8 - ACC_BANKS)
            words = tiles["x_raw", q, c][:].bitcast(F32)
            for i in range(2):
                for u in range(2):
                    nc.tensor.transpose(bank[:, i, u, :], words[:, i, u : 2 * P : 2], ident[:])
            tiles["x_bank", q, c] = bank

        def group_x(q, c):
            grp = work.tile([P, QUARTER * PACK], BF16, name="x_grp", bufs=6, align_bytes=64)
            nc.scalar.copy(
                out=grp[:].bitcast(F32).rearrange("p (i r u) -> p i r u", i=2, u=2),
                in_=tiles["x_bank", q, c][:].rearrange("p i u r -> p i r u"),
            )
            tiles["x_grp", q, c] = grp

        def quant_x(q, c):
            cols = slice(q * QUARTER, (q + 1) * QUARTER)
            nc.vector.quantize_mx(
                out=x_codes[:, c, cols].bitcast(FP8X4), scales=x_scales[:, c, cols], in_=tiles["x_grp", q, c][:]
            )

        def group_w(g, c, engine, m0, m1):
            if ("w_grp", g, c) not in tiles:
                tiles["w_grp", g, c] = work.tile([P, SPAN * PACK], BF16, name="w_grp", bufs=3, align_bytes=64)
            dst = tiles["w_grp", g, c][:].rearrange("p (t a b j) -> p a j b t", t=PACK, j=PACK, b=2)[:, m0 // 2 : m1 // 2]
            src = tiles["w_raw", g, c][:].rearrange("p j (a b t) -> p a j b t", t=PACK, b=2)[:, m0 // 2 : m1 // 2]
            if engine == "vector":
                nc.vector.tensor_copy(out=dst, in_=src)
            else:
                nc.scalar.copy(out=dst, in_=src)

        def quant_w(g, c):
            nc.vector.quantize_mx(
                out=w_codes[:, g, c, :].bitcast(FP8X4), scales=w_scales[:, g, c, :], in_=tiles["w_grp", g, c][:]
            )

        def multiply(u, t, c):
            g, m0, width = UNITS[u]
            if c == 0:
                tiles["acc", u, t] = psum.tile([P, width], F32, name="acc", tag="acc", bufs=ACC_BANKS)
            feats = slice(t * P, (t + 1) * P)
            mols = slice(m0, m0 + width)
            nc.tensor.matmul_mx(
                out=tiles["acc", u, t][:],
                lhsT=w_codes[:, g, c, feats].bitcast(FP8X4),
                lhsT_scale=w_scales[:, g, c, feats],
                rhs=x_codes[:, c, mols].bitcast(FP8X4),
                rhs_scale=x_scales[:, c, mols],
                start=(c == 0),
                stop=(c == PASSES - 1),
            )

        def column(vec, u, t):
            g = UNITS[u][0]
            return vec[:, t // 2, t % 2, g : g + 1]

        def to_turns(s, i):
            u, ts = STEPS[s]
            if i == 0:
                tiles["turns", s] = work.tile([P, len(ts), UNITS[u][2]], F32, name="turns", bufs=3)
            nc.scalar.activation(
                out=tiles["turns", s][:, i, :], in_=tiles["acc", u, ts[i]][:], func=ACT.Identity,
                bias=column(shift, u, ts[i]), scale=column(rate, u, ts[i]),
            )

        def whole_turns(s):
            whole = work.tile(tiles["turns", s].shape, I32, name="whole", bufs=2)
            nc.vector.tensor_copy(out=whole[:], in_=tiles["turns", s][:])
            tiles["whole", s] = whole

        def rest_turns(s):
            rest = work.tile(tiles["turns", s].shape, F32, name="rest", bufs=3)
            nc.vector.tensor_tensor(out=rest[:], in0=tiles["turns", s][:], in1=tiles["whole", s][:], op=ALU.subtract)
            tiles["rest", s] = rest

        def cosine(s):
            wave = work.tile(tiles["rest", s].shape, F32, name="wave", bufs=3)
            nc.scalar.activation(out=wave[:], in_=tiles["rest", s][:], func=ACT.Sin, scale=TWO_PI)
            tiles["wave", s] = wave

        def scale(s):
            u, ts = STEPS[s]
            if ts[0] == 0:
                tiles["y", u] = work.tile([P, PACK, UNITS[u][2]], F32, name="y", bufs=2)
            for i, t in enumerate(ts):
                nc.vector.tensor_scalar(
                    out=tiles["y", u][:, t, :], in0=tiles["wave", s][:, i, :], scalar1=column(gain, u, t),
                    scalar2=None, op0=ALU.mult,
                )

        def turn_y(u, b):
            bank = psum.tile([P, PACK, P], F32, name="turned", tag="turned", bufs=8 - ACC_BANKS)
            for t in range(PACK):
                nc.tensor.transpose(bank[:, t, :], tiles["y", u][:, t, b * P : (b + 1) * P], ident[:])
            tiles["y_bank", u, b] = bank

        def fetch_y(u, b):
            rows = work.tile([P, P, PACK], F32, name="y_rows", bufs=8)
            nc.scalar.copy(out=rows[:], in_=tiles["y_bank", u, b][:].rearrange("m t p -> m p t"))
            g, m0, width = UNITS[u]
            nc.sync.dma_start(
                out=out_0[m0 + b * P : m0 + (b + 1) * P, g * SPAN : (g + 1) * SPAN],
                in_=rows[:].rearrange("m p t -> m (p t)"),
            )

        def group_y(u):
            grp = work.tile([P, UNITS[u][2] * PACK], BF16, name="y_grp", bufs=2, align_bytes=64)
            nc.vector.tensor_copy(
                out=grp[:].rearrange("p (c i t) -> p c t i", i=4, t=PACK),
                in_=tiles["y", u][:].rearrange("p t (c i) -> p c t i", i=4),
            )
            tiles["y_grp", u] = grp

        def quant_y(u):
            g, m0, width = UNITS[u]
            mols = slice(m0, m0 + width)
            codes = work.tile([P, width], U32, name="y_codes", bufs=3, align_bytes=64)
            nc.vector.quantize_mx(out=codes[:].bitcast(FP8X4), scales=y_scales[:, g, mols], in_=tiles["y_grp", u][:])
            dst = out_1[g].rearrange("p m t -> p (m t)").bitcast(I32)
            nc.sync.dma_start(out=dst[:, mols], in_=codes[:].bitcast(I32))

        def store_scales(g0, g1, queue):
            for q in range(4):
                queue.dma_start(
                    out=out_2[g0:g1, 4 * q : 4 * q + 4, :].rearrange("g r m -> r g m").bitcast(I32),
                    in_=y_scales[32 * q : 32 * q + 4, g0:g1, :].bitcast(I32),
                )

        vec_rows = keep.tile([P, SPAN], BF16, name="vec_rows")
        nc.vector.memset(vec_rows[:], 0.0)
        for c in range(PASSES):
            load_x(0, c)
            load_w(0, c)
            vec = (inv_length, phase, amp)[c]
            nc.sync.dma_start(
                out=vec_rows[c * GROUPS : (c + 1) * GROUPS, :], in_=vec.rearrange("(g n) -> g n", g=GROUPS)
            )
        for load, part in ((load_x, 1), (load_w, 1), (load_x, 2), (load_x, 3), (load_w, 2), (load_w, 3)):
            for c in range(PASSES):
                load(part, c)

        ident = keep.tile([P, P], F32, name="ident")
        make_identity(nc, ident[:])
        warm = keep.tile([P, 1], F32, name="warm")
        nc.scalar.activation(out=warm[:], in_=ident[:, 0:1], func=ACT.Sin)

        rate = keep.tile([P, 2, 2, GROUPS], F32, name="rate")
        shift = keep.tile([P, 2, 2, GROUPS], F32, name="shift")
        gain = keep.tile([P, 2, 2, GROUPS], F32, name="gain")

        def spread_vectors():
            bank = psum.tile([P, 2, P], F32, name="turned", tag="turned", bufs=8 - ACC_BANKS)
            words = vec_rows[:].bitcast(F32)
            for u in range(2):
                nc.tensor.transpose(bank[:, u, :], words[:, u : 2 * P : 2], ident[:])
            cols = bank[:].bitcast(BF16).rearrange("p u (r e) -> p u e r", e=2)
            nc.vector.tensor_scalar(
                out=rate[:], in0=cols[:, :, :, 0:GROUPS], scalar1=1.0 / TWO_PI, scalar2=None, op0=ALU.mult
            )
            nc.vector.tensor_scalar(
                out=shift[:], in0=cols[:, :, :, GROUPS : 2 * GROUPS], scalar1=1.0 / TWO_PI, scalar2=0.25,
                op0=ALU.mult, op1=ALU.add,
            )
            nc.vector.tensor_copy(out=gain[:], in_=cols[:, :, :, 2 * GROUPS : 3 * GROUPS])

        for c in range(PASSES):
            turn_x(0, c)
            if c == PASSES - 1:
                spread_vectors()
            group_x(0, c)
            group_w(0, c, "vector", 0, HEAD_SPLIT[c])
            group_w(0, c, "scalar", HEAD_SPLIT[c], P)
            quant_x(0, c)
            quant_w(0, c)
        for c in range(PASSES):
            for t in range(ACC_BANKS):
                multiply(0, t, c)
        for c in range(PASSES):
            turn_x(1, c)
            group_x(1, c)
            quant_x(1, c)

        order = [(u, t) for u in range(len(UNITS)) for t in range(PACK)]
        steps = len(STEPS)
        ends = {s: u for s, (u, ts) in enumerate(STEPS) if ts[-1] == PACK - 1}
        for s in range(steps + 5):
            if s - 4 in ends:
                u = ends[s - 4]
                for b in range(UNITS[u][2] // P):
                    turn_y(u, b)
                    fetch_y(u, b)
                group_y(u)
            for q, c in X_STEP.get(s, []):
                turn_x(q, c)
                group_x(q, c)
                quant_x(q, c)
            for g, c, split in W_STEP.get(s, []):
                group_w(g, c, "vector", 0, split)
                group_w(g, c, "scalar", split, P)
                quant_w(g, c)
            if s < steps:
                for i, t in enumerate(STEPS[s][1]):
                    to_turns(s, i)
                    ahead = STEPS[s][0] * PACK + t + ACC_BANKS
                    if ahead < len(order):
                        for c in range(PASSES):
                            multiply(order[ahead][0], order[ahead][1], c)
            if 2 <= s < steps + 2:
                cosine(s - 2)
            if 1 <= s <= steps:
                whole_turns(s - 1)
            if 3 <= s < steps + 3:
                scale(s - 3)
            if 1 <= s <= steps:
                rest_turns(s - 1)
            if s - 5 in ends:
                quant_y(ends[s - 5])
            if s == steps + 2:
                store_scales(0, GROUPS - 1, nc.sync)
        store_scales(GROUPS - 1, GROUPS, nc.scalar)
